import numpy as np
import ml_dtypes


def mxq(x, axis, fmt="e4m3"):
    dtype, down = {"e4m3": (ml_dtypes.float8_e4m3fn, 7), "e5m2": (ml_dtypes.float8_e5m2, 14)}[fmt]
    v = np.moveaxis(np.asarray(x, np.float32).astype(ml_dtypes.bfloat16).astype(np.float64), axis, -1)
    blocks = v.reshape(v.shape[:-1] + (-1, 32))
    amax = np.abs(blocks).max(-1, keepdims=True)
    byte = np.maximum(np.where(amax > 0, np.frexp(amax)[1] - 1 + 127, 0) - down, 1)
    scale = np.exp2(byte - 127.0)
    codes = (blocks / scale).astype(np.float32).astype(dtype).astype(np.float64)
    return np.moveaxis((codes * scale).reshape(v.shape), -1, axis)


WIDE = False


def mx_kscale(k):
    if not WIDE:
        return np.ones(k)
    levels = np.array([10, -10, 5, -5, 0])
    if k % 512:
        return np.exp2(np.random.permutation(np.resize(levels, k // 32))).repeat(32)
    a = np.empty((k // 512, 16))
    for p in range(k // 512):
        a[p, :8] = np.random.permutation(np.resize(levels, 8))
        for g in range(8):
            far = levels[np.abs(levels - a[p, g]) >= 10]
            a[p, g + 8] = far[np.random.randint(len(far))]
    return np.exp2(a.ravel()).repeat(32)


BF16 = ml_dtypes.bfloat16


def bf(x):
    return np.asarray(x, np.float32).astype(BF16)


def f64(x):
    return np.asarray(x).astype(np.float64)


E2M1 = np.array([0.0, 0.5, 1.0, 1.5, 2.0, 3.0, 4.0, 6.0, -0.0, -0.5, -1.0, -1.5, -2.0, -3.0, -4.0, -6.0])


def pack_weight(w, fmt):
    k, n = w.shape
    w = f64(bf(w)).reshape(k // 32, 32, n)
    amax = np.abs(w).max(1)
    if fmt == "e4m3":
        byte = np.frexp(amax)[1] - 1 + 127 - 7
    else:
        mant, ex = np.frexp(amax / 6.0)
        byte = np.where(mant > 0.5, ex, ex - 1) + 127
    byte = np.clip(np.where(amax > 0, byte, 1), 1, 254)
    scaled = (w * np.exp2(127.0 - byte)[:, None, :]).reshape(k, n).astype(np.float32)
    by_word = np.ascontiguousarray(scaled.reshape(k // 512, 128, 4, n).transpose(0, 1, 3, 2))
    if fmt == "e4m3":
        words = by_word.astype(ml_dtypes.float8_e4m3fn).view(np.uint8)
    else:
        c = by_word.astype(ml_dtypes.float4_e2m1fn).view(np.uint8) & 0xF
        words = c[..., 0::2] | (c[..., 1::2] << 4)
    return np.ascontiguousarray(words), np.ascontiguousarray(byte.astype(np.uint8).reshape(k // 512, 16, n))


def unpack_weight(words, scales, fmt):
    g, p, n, _ = words.shape
    if fmt == "e4m3":
        vals = np.ascontiguousarray(words).view(ml_dtypes.float8_e4m3fn).astype(np.float64)
    else:
        nib = np.empty((g, p, n, 4), np.uint8)
        nib[..., 0::2] = words & 0xF
        nib[..., 1::2] = words >> 4
        vals = E2M1[nib]
    vals = vals * np.repeat(np.exp2(scales.astype(np.float64) - 127.0), 8, axis=1)[..., None]
    return vals.transpose(0, 1, 3, 2).reshape(g * 512, n)
def pack4(w):
    words, scales = pack_weight(w, "e2m1")
    return words.reshape(words.shape[0], 128, -1), scales


def unpack4(words, scales):
    return unpack_weight(words.reshape(words.shape[0], 128, -1, 2), scales, "e2m1")


def planes(Y):
    n, m = Y.shape
    b = f64(bf(Y)).reshape(n // 32, 32, m)
    amax = np.abs(b).max(1)
    byte = np.clip(np.where(amax > 0, np.frexp(amax)[1] - 1 + 127 - 7, 1), 1, 254)
    codes = (b * np.exp2(127.0 - byte)[:, None, :]).reshape(n, m).astype(np.float32).astype(ml_dtypes.float8_e4m3fn).view(np.uint8)
    words = codes.reshape(n // 512, 128, 4, m).transpose(0, 1, 3, 2)
    return np.ascontiguousarray(words), np.ascontiguousarray(byte.astype(np.uint8).reshape(n // 512, 16, m))


B, S, D, V = 4, 512, 1024, 1024


def sigmoid(v):
    return 1.0 / (1.0 + np.exp(-v))


def setup_inputs():
    a = mx_kscale(D)
    r = mx_kscale(S)
    x = bf(np.random.standard_normal((B, S, D)) * a)
    wf_words, wf_scales = pack4(np.random.standard_normal((D, S)) / np.sqrt(D) / a[:, None])
    rnd = bf(np.random.standard_normal((S, S)))
    wa = bf(np.random.standard_normal(D) / np.sqrt(D) / a)
    wv_words, wv_scales = pack4(np.random.standard_normal((D, V)) / np.sqrt(D) / a[:, None])
    return {
        "x": x,
        "wf_words": wf_words,
        "wf_scales": wf_scales,
        "rnd": rnd,
        "wa": wa,
        "wv_words": wv_words,
        "wv_scales": wv_scales,
        "u": bf((1.0 + 0.1 * np.random.standard_normal(S)) * r),
        "t": bf((1.0 + 0.1 * np.random.standard_normal(S)) / r),
    }


def mixed_logits(x, xq, wf, rnd, wa):
    f = xq @ wf
    al = sigmoid(np.sum(x * wa[None, None, :], axis=-1))
    g = al[:, :, None]
    return 2.0 * (g * f + (1.0 - g) * rnd[None, :, :])


def core(x, wf_words, wf_scales, rnd, wa, wv_words, wv_scales, u, t):
    x, rnd, wa, u, t = f64(x), f64(rnd), f64(wa), f64(u), f64(t)
    wf = unpack4(wf_words, wf_scales)
    wv = unpack4(wv_words, wv_scales)
    xq = mxq(x, 2, "e4m3")
    l = mixed_logits(x, xq, wf, rnd, wa)
    e = np.exp(l - l.max(axis=-1, keepdims=True))
    p = e / e.sum(axis=-1, keepdims=True)
    c = (S * p - 1.0) * u[None, None, :]
    h = xq @ wv
    vv = h * t[None, :, None]
    return (mxq(c, 2, "e4m3") @ mxq(vv, 1, "e4m3")) / np.sqrt(S)


def reference(x, wf_words, wf_scales, rnd, wa, wv_words, wv_scales, u, t):
    R_out = core(x, wf_words, wf_scales, rnd, wa, wv_words, wv_scales, u, t)
    words, scales = planes(np.moveaxis(R_out, 2, 0).reshape(1024, -1))
    return R_out, words, scales

@@ -1,0 +1,392 @@
+import math
+from contextlib import ExitStack
+
+import concourse.mybir as mybir
+from concourse.masks import make_identity
+
+B, S, D, V = 4, 512, 1024, 1024
+FLOPS = 2 * B * S * (D * S + D * V + S * V)
+
+F32 = mybir.dt.float32
+BF16 = mybir.dt.bfloat16
+U32 = mybir.dt.uint32
+I32 = mybir.dt.int32
+U8 = mybir.dt.uint8
+FP8X4 = mybir.dt.float8_e4m3fn_x4
+FP4X4 = mybir.dt.float4_e2m1fn_x4
+ALU = mybir.AluOpType
+ACT = mybir.ActivationFunctionType
+
+P = 128
+PACK = 4
+KP = 512
+NT = B * PACK
+BANKS = 8
+GATE_CLAMP = 44.0
+STEP = [
+    ("X", 0), ("C", 7), ("H0", 6), ("rc", 6), ("mx", 5), ("ge", 1), ("H1", 6), ("cf", 7), ("v0", 6), ("F", 4), ("xc", 0), ("og1", 14), ("k0", 9), ("st", 11), ("ps1", 15), ("gd", 1), ("v1", 6), ("og0", 11), ("O1", 10), ("ex", 5), ("e1", 10), ("gr", 1), ("y", 4), ("O0", 8), ("cq", 7), ("G", 0), ("xq", 0), ("vq", 6), ("T1", 13), ("T0", 10), ("gc", 0), ("ps0", 12), ("e0", 8), ("oq0", 11), ("k1", 10), ("w", 6), ("oq1", 14)
+]
+ENGINES = {
+    "w": "GGGGGGGGGGGGGGGG",
+    "xc": "AAAAAAAAAAAAAAAA",
+    "og0": "AAAAAAAAAAAAADDA",
+    "og1": "AAAAAAAAAAAAAAAA",
+    "e0": "AAAAAAAAAAAAAAAD",
+    "k1": "AAAAAAAAAAADDDDD",
+    "e1": "AAAAAAAAAAAAAAAA",
+    "k0": "AAAAAAAAAAAAADDD"
+}
+
+
+def tile_tokengatedmixtureofsynthesizers_x2_kernel(
+    tc, x, wf_words, wf_scales, rnd, wa, wv_words, wv_scales, u, t, out_0, out_1, out_2
+):
+    nc = tc.nc
+    with ExitStack() as ctx:
+        keep = ctx.enter_context(tc.tile_pool(name="keep", bufs=1))
+        work = ctx.enter_context(tc.tile_pool(name="work", bufs=3))
+        psum = ctx.enter_context(tc.psum_pool(name="psum", bufs=1))
+        ctx.enter_context(tc.manual_schedule())
+
+        def copy_on(kind, n, out, in_):
+            if ENGINES[kind][n] == "D":
+                nc.vector.tensor_copy(out=out, in_=in_)
+            elif ENGINES[kind][n] == "G":
+                nc.gpsimd.tensor_scalar(out=out, in0=in_, scalar1=1.0, scalar2=0.0, op0=ALU.mult, op1=ALU.add)
+            else:
+                nc.scalar.copy(out=out, in_=in_)
+
+        bank_count = [0]
+
+        def next_bank():
+            k = bank_count[0] % BANKS
+            bank_count[0] += 1
+            return psum.tile([P, KP], F32, name="bank%d" % k)
+
+        ident = keep.tile([P, P], F32, name="ident")
+        make_identity(nc, ident[:])
+        wf_s = keep.tile([P, 2, S], U8, name="wf_s", align_bytes=64)
+        wv_s = keep.tile([P, 2, V], U8, name="wv_s", align_bytes=64)
+        nc.vector.memset(wf_s[:].rearrange("p g n -> p (g n)").bitcast(I32), 0)
+        nc.vector.memset(wv_s[:].rearrange("p g n -> p (g n)").bitcast(I32), 0)
+
+        x_sb = {}
+
+        def load_x(b, t0, n):
+            xt = keep.tile([P, n, D], BF16, name="x_%d_%d" % (b, t0))
+            nc.sync.dma_start(out=xt[:], in_=x[b].rearrange("(m t) d -> m t d", t=PACK)[:, t0 : t0 + n, :])
+            for k in range(n):
+                x_sb[PACK * b + t0 + k] = xt[:, k, :]
+
+        wa_sb = keep.tile([P, 2, PACK], BF16, name="wa_sb")
+        u_sb = keep.tile([P, PACK], BF16, name="u_sb")
+        t_sb = keep.tile([P, PACK], BF16, name="t_sb")
+        wf_w = keep.tile([P, 2, 2 * S], U8, name="wf_w", align_bytes=64)
+        wv_w = keep.tile([P, 2, 2 * V], U8, name="wv_w", align_bytes=64)
+        rnd_sb = keep.tile([P, PACK, S], BF16, name="rnd_sb")
+
+        for k in range(PACK):
+            load_x(0, k, 1)
+        nc.scalar.dma_start(out=wa_sb[:], in_=wa.rearrange("(g p t) -> p g t", g=2, t=PACK))
+        for q in range(4):
+            nc.scalar.dma_start(
+                out=wf_s[32 * q : 32 * q + 4, :, :].bitcast(I32),
+                in_=wf_scales[:, 4 * q : 4 * q + 4, :].rearrange("g r n -> r g n").bitcast(I32),
+            )
+        for q in range(4):
+            nc.scalar.dma_start(
+                out=wv_s[32 * q : 32 * q + 4, :, :].bitcast(I32),
+                in_=wv_scales[:, 4 * q : 4 * q + 4, :].rearrange("g r n -> r g n").bitcast(I32),
+            )
+        nc.scalar.dma_start(out=t_sb[:], in_=t.rearrange("(p t) -> p t", t=PACK))
+        nc.scalar.dma_start(out=u_sb[:], in_=u.rearrange("(p t) -> p t", t=PACK))
+        nc.sync.dma_start(out=wf_w[:].bitcast(I32), in_=wf_words.rearrange("g p n -> p g n").bitcast(I32))
+        nc.sync.dma_start(out=wv_w[:].bitcast(I32), in_=wv_words.rearrange("g p n -> p g n").bitcast(I32))
+        nc.sync.dma_start(out=rnd_sb[:], in_=rnd.rearrange("(m t) j -> m t j", t=PACK))
+        for b in range(1, B):
+            load_x(b, 0, 2)
+            load_x(b, 2, 2)
+
+        warm = keep.tile([P, 1], F32, name="warm")
+        nc.scalar.activation(out=warm[:], in_=ident[:, 0:1], func=ACT.Exp)
+        u512 = keep.tile([P, PACK], F32, name="u512")
+        nc.gpsimd.tensor_scalar(out=u512[:], in0=u_sb[:], scalar1=float(S), scalar2=0.0, op0=ALU.mult, op1=ALU.add)
+
+        xg, xq, xs = {}, {}, {}
+        rho, nsg, zneg = {}, {}, {}
+        banks = {}
+        y, nl, nm, e, esum, rinv, w = {}, {}, {}, {}, {}, {}, {}
+        cg, cq, cs = {}, {}, {}
+        vg, vq, vs = {}, {}, {}
+        o32, ob, og, oq, osc = {}, {}, {}, {}, {}
+
+        def x_transpose(n):
+            bk = next_bank()
+            banks["x", n] = bk
+            words = x_sb[n].bitcast(F32)
+            for g in range(2):
+                for h in range(2):
+                    c0 = (2 * g + h) * P
+                    nc.tensor.transpose(bk[:, c0 : c0 + P], words[:, 256 * g + h : 256 * (g + 1) : 2], ident[:])
+
+        def x_copy(n):
+            xg[n] = work.tile([P, 2 * P * PACK], BF16, name="xg", bufs=8, align_bytes=64)
+            copy_on(
+                "xc", n,
+                out=xg[n][:].bitcast(F32).rearrange("p (g m h) -> p g m h", g=2, h=2),
+                in_=banks["x", n][:].rearrange("p (g h m) -> p g m h", g=2, h=2),
+            )
+
+        def x_quant(n):
+            xq[n] = work.tile([P, 2 * P], U32, name="xq", bufs=12, align_bytes=64)
+            xs[n] = work.tile([P, 2 * P], U8, name="xs", bufs=12, align_bytes=64)
+            nc.vector.quantize_mx(out=xq[n][:].bitcast(FP8X4), scales=xs[n][:], in_=xg[n][:])
+
+        def gate_mm(b):
+            bk = next_bank()
+            banks["g", b] = bk
+            for k in range(PACK):
+                xv = xg[PACK * b + k][:].rearrange("p (g m t) -> p g t m", g=2, t=PACK)
+                for g in range(2):
+                    for j in range(PACK):
+                        nc.tensor.matmul(
+                            out=bk[:, k : k + 1],
+                            lhsT=xv[:, g, j, :],
+                            rhs=wa_sb[:, g, j : j + 1],
+                            start=(g == 0 and j == 0),
+                            stop=(g == 1 and j == PACK - 1),
+                        )
+
+        def gate_clamp(b):
+            zneg[b] = work.tile([P, PACK], F32, name="zneg", bufs=2)
+            nc.vector.tensor_scalar(
+                out=zneg[b][:], in0=banks["g", b][:, 0:PACK], scalar1=-1.0, scalar2=GATE_CLAMP, op0=ALU.mult, op1=ALU.min
+            )
+
+        def gate_exp(b):
+            rho[b] = work.tile([P, PACK], F32, name="rho", bufs=2)
+            nc.scalar.activation(out=rho[b][:], in_=zneg[b][:], func=ACT.Exp)
+
+        def gate_den(b):
+            zneg[b] = work.tile([P, PACK], F32, name="gden", bufs=2)
+            nc.vector.tensor_scalar(
+                out=zneg[b][:], in0=rho[b][:], scalar1=-0.5, scalar2=-0.5, op0=ALU.mult, op1=ALU.add
+            )
+
+        def gate_recip(b):
+            nsg[b] = work.tile([P, PACK], F32, name="nsg", bufs=2)
+            nc.vector.reciprocal(out=nsg[b][:], in_=zneg[b][:])
+
+        def f_mm(n):
+            bk = next_bank()
+            banks["f", n] = bk
+            for g in range(2):
+                nc.tensor.matmul_mx(
+                    out=bk[:],
+                    lhsT=xq[n][:, g * P : (g + 1) * P].bitcast(FP8X4),
+                    lhsT_scale=xs[n][:, g * P : (g + 1) * P],
+                    rhs=wf_w[:, g, :].bitcast(FP4X4),
+                    rhs_scale=wf_s[:, g, :],
+                    start=(g == 0),
+                    stop=(g == 1),
+                )
+
+        def mix(n):
+            b, k = divmod(n, PACK)
+            y[n] = work.tile([P, S], F32, name="y", bufs=3)
+            nc.vector.scalar_tensor_tensor(
+                out=y[n][:].rearrange("q (j p) -> q j p", j=PACK),
+                in0=rnd_sb[:, k, :].rearrange("q (p j) -> q j p", j=PACK),
+                scalar=rho[b][:, k : k + 1],
+                in1=banks["f", n][:].rearrange("q (p j) -> q j p", j=PACK),
+                op0=ALU.mult,
+                op1=ALU.add,
+            )
+
+        def row_max(n):
+            b, k = divmod(n, PACK)
+            nl[n] = work.tile([P, S], F32, name="nl", bufs=3)
+            nm[n] = work.tile([P, 1], F32, name="nm", bufs=3)
+            nc.vector.tensor_scalar(
+                out=nl[n][:], in0=y[n][:], scalar1=nsg[b][:, k : k + 1], scalar2=None,
+                op0=ALU.mult, op1=ALU.min, accum_out=nm[n][:],
+            )
+
+        def exp_sum(n):
+            e[n] = work.tile([P, S], F32, name="e", bufs=3)
+            esum[n] = work.tile([P, 1], F32, name="esum", bufs=3)
+            nc.scalar.activation(out=e[n][:], in_=nl[n][:], func=ACT.Exp, bias=nm[n][:], scale=-1.0, accum_out=esum[n][:])
+
+        def sum_recip(n):
+            rinv[n] = work.tile([P, 1], F32, name="rinv", bufs=3)
+            nc.vector.reciprocal(out=rinv[n][:], in_=esum[n][:])
+
+        def normalise(n):
+            w[n] = work.tile([P, S], F32, name="w", bufs=3)
+            if ENGINES["w"][n] == "G":
+                nc.gpsimd.tensor_scalar(
+                    out=w[n][:], in0=e[n][:], scalar1=rinv[n][:], scalar2=0.0, op0=ALU.mult, op1=ALU.add
+                )
+            elif ENGINES["w"][n] == "D":
+                nc.vector.tensor_scalar(out=w[n][:], in0=e[n][:], scalar1=rinv[n][:], scalar2=None, op0=ALU.mult)
+            else:
+                nc.scalar.activation(out=w[n][:], in_=e[n][:], func=ACT.Copy, scale=rinv[n][:])
+
+        def c_transpose(n):
+            bk = next_bank()
+            banks["c", n] = bk
+            for j in range(PACK):
+                nc.tensor.transpose(bk[:, j * P : (j + 1) * P], w[n][:, j * P : (j + 1) * P], ident[:])
+
+        def c_form(n):
+            cg[n] = work.tile([P, P * PACK], BF16, name="cg", bufs=3, align_bytes=64)
+            nc.vector.scalar_tensor_tensor(
+                out=cg[n][:].rearrange("p (i j) -> p i j", j=PACK),
+                in0=banks["c", n][:].rearrange("p (j i) -> p i j", j=PACK),
+                scalar=1.0 / S,
+                in1=u512[:].unsqueeze(1).broadcast_to([P, P, PACK]),
+                op0=ALU.subtract,
+                op1=ALU.mult,
+            )
+
+        def c_quant(n):
+            cq[n] = work.tile([P, P], U32, name="cq", bufs=6, align_bytes=64)
+            cs[n] = work.tile([P, P], U8, name="cs", bufs=6, align_bytes=64)
+            nc.vector.quantize_mx(out=cq[n][:].bitcast(FP8X4), scales=cs[n][:], in_=cg[n][:])
+
+        def h_mm(b, k):
+            bk = next_bank()
+            banks["h", b, k] = bk
+            for j in range(PACK):
+                n = PACK * b + j
+                for g in range(2):
+                    nc.tensor.matmul_mx(
+                        out=bk[:, j * P : (j + 1) * P],
+                        lhsT=xq[n][:, g * P : (g + 1) * P].bitcast(FP8X4),
+                        lhsT_scale=xs[n][:, g * P : (g + 1) * P],
+                        rhs=wv_w[:, g, 2 * P * k : 2 * P * (k + 1)].bitcast(FP4X4),
+                        rhs_scale=wv_s[:, g, P * k : P * (k + 1)],
+                        start=(g == 0),
+                        stop=(g == 1),
+                    )
+
+        def v_form(b, k):
+            half, kk = divmod(k, PACK)
+            if (b, half) not in vg:
+                vg[b, half] = work.tile([P, KP * PACK], BF16, name="vg", bufs=3, align_bytes=64)
+            nc.vector.tensor_tensor(
+                out=vg[b, half][:, kk * KP : (kk + 1) * KP].rearrange("p (m j) -> p m j", j=PACK),
+                in0=banks["h", b, k][:].rearrange("p (j m) -> p m j", j=PACK),
+                in1=t_sb[:].unsqueeze(1).broadcast_to([P, P, PACK]),
+                op=ALU.mult,
+            )
+
+        def v_quant(b, half):
+            vq[b, half] = work.tile([P, KP], U32, name="vq", bufs=5, align_bytes=64)
+            vs[b, half] = work.tile([P, KP], U8, name="vs", bufs=5, align_bytes=64)
+            nc.vector.quantize_mx(out=vq[b, half][:].bitcast(FP8X4), scales=vs[b, half][:], in_=vg[b, half][:])
+
+        def o_mm(n, half):
+            b = n // PACK
+            bk = next_bank()
+            banks["o", n, half] = bk
+            nc.tensor.matmul_mx(
+                out=bk[:],
+                lhsT=cq[n][:].bitcast(FP8X4),
+                lhsT_scale=cs[n][:],
+                rhs=vq[b, half][:].bitcast(FP8X4),
+                rhs_scale=vs[b, half][:],
+                start=True,
+                stop=True,
+            )
+
+        def o_evac(n, half):
+            if n not in o32:
+                o32[n] = work.tile([P, V], F32, name="o32", bufs=6)
+            dst = o32[n][:, half * KP : (half + 1) * KP]
+            if ENGINES["e%d" % half][n] == "D":
+                nc.vector.tensor_scalar(
+                    out=dst, in0=banks["o", n, half][:], scalar1=1.0 / math.sqrt(S), scalar2=None, op0=ALU.mult
+                )
+            else:
+                nc.scalar.activation(out=dst, in_=banks["o", n, half][:], func=ACT.Copy, scale=1.0 / math.sqrt(S))
+
+        def o_store(n):
+            b, k = divmod(n, PACK)
+            nc.sync.dma_start(out=out_0[b].rearrange("(m t) v -> m t v", t=PACK)[:, k, :], in_=o32[n][:])
+
+        def o_cast(n, half):
+            ob[n, half] = work.tile([P, KP], BF16, name="ob", bufs=8)
+            copy_on(
+                "k%d" % half, n,
+                out=ob[n, half][:].rearrange("q (h p e) -> q h p e", h=2, e=2),
+                in_=o32[n][:, half * KP : (half + 1) * KP].rearrange("q (p h e) -> q h p e", h=2, e=2),
+            )
+
+        def o_transpose(pair, g):
+            bk = next_bank()
+            banks["t", pair, g] = bk
+            for a in range(2):
+                words = ob[2 * pair + a, g][:].bitcast(F32)
+                for h in range(2):
+                    c0 = (2 * a + h) * P
+                    nc.tensor.transpose(bk[:, c0 : c0 + P], words[:, h * P : (h + 1) * P], ident[:])
+
+        def o_gather(pair, g):
+            b, pp = divmod(pair, 2)
+            if pp == 0:
+                og[b, g] = work.tile([P, S * PACK], BF16, name="og", bufs=4, align_bytes=64)
+            copy_on(
+                "og%d" % g, 2 * pair + 1,
+                out=og[b, g][:].bitcast(F32).rearrange("p (m c) -> p m c", c=8)[:, :, 4 * pp : 4 * pp + 4],
+                in_=banks["t", pair, g][:].rearrange("p (c m) -> p m c", c=4),
+            )
+
+        def o_quant(b, g):
+            oq[b, g] = work.tile([P, S], U32, name="oq", bufs=3, align_bytes=64)
+            if b not in osc:
+                osc[b] = work.tile([P, 2, S], U8, name="osc", bufs=2, align_bytes=64)
+            nc.vector.quantize_mx(out=oq[b, g][:].bitcast(FP8X4), scales=osc[b][:, g, :], in_=og[b, g][:])
+
+        def plane_store(b, g):
+            cols = slice(b * S, (b + 1) * S)
+            nc.sync.dma_start(
+                out=out_1[g, :, cols, :].rearrange("p n t -> p (n t)").bitcast(I32), in_=oq[b, g][:].bitcast(I32)
+            )
+            if g == 1:
+                for q in range(4):
+                    nc.sync.dma_start(
+                        out=out_2[:, 4 * q : 4 * q + 4, cols].rearrange("g r n -> r g n").bitcast(I32),
+                        in_=osc[b][32 * q : 32 * q + 4, :, :].bitcast(I32),
+                    )
+
+        every_tile = {
+            "X": x_transpose, "xc": x_copy, "xq": x_quant, "F": f_mm, "y": mix, "mx": row_max, "ex": exp_sum,
+            "rc": sum_recip, "w": normalise, "C": c_transpose, "cf": c_form, "cq": c_quant, "st": o_store,
+            "H0": lambda n: h_mm(n // PACK, 2 * (n % PACK)), "H1": lambda n: h_mm(n // PACK, 2 * (n % PACK) + 1),
+            "v0": lambda n: v_form(n // PACK, 2 * (n % PACK)), "v1": lambda n: v_form(n // PACK, 2 * (n % PACK) + 1),
+            "O0": lambda n: o_mm(n, 0), "O1": lambda n: o_mm(n, 1),
+            "e0": lambda n: o_evac(n, 0), "e1": lambda n: o_evac(n, 1),
+            "k0": lambda n: o_cast(n, 0), "k1": lambda n: o_cast(n, 1),
+        }
+        every_pair = {
+            "vq": lambda n: v_quant(n // PACK, (n % PACK) // 2),
+            "T0": lambda n: o_transpose(n // 2, 0), "T1": lambda n: o_transpose(n // 2, 1),
+            "og0": lambda n: o_gather(n // 2, 0), "og1": lambda n: o_gather(n // 2, 1),
+        }
+        every_batch = {
+            "G": gate_mm, "gc": gate_clamp, "ge": gate_exp, "gd": gate_den, "gr": gate_recip,
+            "oq0": lambda b: o_quant(b, 0), "oq1": lambda b: o_quant(b, 1),
+            "ps0": lambda b: plane_store(b, 0), "ps1": lambda b: plane_store(b, 1),
+        }
+        for s in range(NT + max(lag for name, lag in STEP)):
+            for name, lag in STEP:
+                n = s - lag
+                if not 0 <= n < NT:
+                    continue
+                if name in every_tile:
+                    every_tile[name](n)
+                elif name in every_pair and n % 2 == 1:
+                    every_pair[name](n)
+                elif name in every_batch and n % PACK == PACK - 1:
+                    every_batch[name](n // PACK)

@@ -22,19 +22,60 @@ PACK = 4
 KP = 512
 NT = B * PACK
 BANKS = 8
-GATE_CLAMP = 44.0
+RHO_MAX = 2.0**64
+GATE_N = 64
 STEP = [
-    ("X", 0), ("C", 7), ("H0", 6), ("rc", 6), ("mx", 5), ("ge", 1), ("H1", 6), ("cf", 7), ("v0", 6), ("F", 4), ("xc", 0), ("og1", 14), ("k0", 9), ("st", 11), ("ps1", 15), ("gd", 1), ("v1", 6), ("og0", 11), ("O1", 10), ("ex", 5), ("e1", 10), ("gr", 1), ("y", 4), ("O0", 8), ("cq", 7), ("G", 0), ("xq", 0), ("vq", 6), ("T1", 13), ("T0", 10), ("gc", 0), ("ps0", 12), ("e0", 8), ("oq0", 11), ("k1", 10), ("w", 6), ("oq1", 14)
+    ("X", (0, 0, 0, 0)),
+    ("v1", (3, 3, 3, 3)),
+    ("C", (8, 8, 8, 8)),
+    ("og1", (13, 13, 13, 13)),
+    ("T0", (11, 11, 11, 11)),
+    ("cf", (8, 8, 8, 8)),
+    ("oq0", (13, 13, 13, 13)),
+    ("xc", (0, 0, 0, 0)),
+    ("il", (6, 6, 6, 6)),
+    ("xq", (0, 0, 0, 0)),
+    ("ps0", (14, 14, 14, 14)),
+    ("G", (1, 1, 1, 1)),
+    ("k0", (10, 10, 10, 10)),
+    ("vq1", (6, 6, 6, 6)),
+    ("O1", (10, 10, 10, 10)),
+    ("k1", (11, 11, 11, 11)),
+    ("O0", (9, 9, 9, 9)),
+    ("og0", (11, 11, 11, 11)),
+    ("ge", (1, 1, 1, 1)),
+    ("F", (4, 4, 4, 4)),
+    ("vq0", (5, 5, 5, 5)),
+    ("oq1", (15, 15, 15, 15)),
+    ("st", (11, 11, 11, 11)),
+    ("gc", (1, 1, 1, 1)),
+    ("rc", (6, 6, 6, 6)),
+    ("cq", (8, 8, 8, 8)),
+    ("y", (4, 4, 4, 4)),
+    ("H0", (4, 4, 4, 4)),
+    ("gd", (1, 1, 1, 1)),
+    ("e1", (10, 10, 10, 10)),
+    ("H1", (2, 2, 2, 2)),
+    ("gr", (1, 1, 1, 1)),
+    ("w", (6, 6, 6, 6)),
+    ("v0", (4, 4, 4, 4)),
+    ("e0", (9, 9, 9, 9)),
+    ("ps1", (15, 15, 15, 15)),
+    ("mx", (4, 4, 4, 4)),
+    ("ex", (5, 5, 5, 5)),
+    ("T1", (12, 12, 12, 12))
 ]
 ENGINES = {
     "w": "GGGGGGGGGGGGGGGG",
     "xc": "AAAAAAAAAAAAAAAA",
-    "og0": "AAAAAAAAAAAAADDA",
-    "og1": "AAAAAAAAAAAAAAAA",
-    "e0": "AAAAAAAAAAAAAAAD",
-    "k1": "AAAAAAAAAAADDDDD",
+    "v1": "AAAAAAAAAAAAAAAA",
+    "il": "AAGGAAAAAAAAAAAA",
+    "e0": "AAAAAAAAAAAAAAAA",
     "e1": "AAAAAAAAAAAAAAAA",
-    "k0": "AAAAAAAAAAAAADDD"
+    "k0": "GGGGGGGGGGGDADDD",
+    "k1": "GGGGGGGGGGDDDDDD",
+    "og0": "AAAAAAAAAAAADDAA",
+    "og1": "AAAAAAAAAAAAAAAA"
 }
 
 
@@ -65,10 +106,12 @@ def tile_tokengatedmixtureofsynthesizers_x2_kernel(
 
         ident = keep.tile([P, P], F32, name="ident")
         make_identity(nc, ident[:])
+        wa_sb = keep.tile([P, 2 * PACK + GATE_N], BF16, name="wa_sb")
+        nc.vector.memset(wa_sb[:].bitcast(I32), 0)
         wf_s = keep.tile([P, 2, S], U8, name="wf_s", align_bytes=64)
         wv_s = keep.tile([P, 2, V], U8, name="wv_s", align_bytes=64)
-        nc.vector.memset(wf_s[:].rearrange("p g n -> p (g n)").bitcast(I32), 0)
         nc.vector.memset(wv_s[:].rearrange("p g n -> p (g n)").bitcast(I32), 0)
+        nc.vector.memset(wf_s[:].rearrange("p g n -> p (g n)").bitcast(I32), 0)
 
         x_sb = {}
 
@@ -78,42 +121,51 @@ def tile_tokengatedmixtureofsynthesizers_x2_kernel(
             for k in range(n):
                 x_sb[PACK * b + t0 + k] = xt[:, k, :]
 
-        wa_sb = keep.tile([P, 2, PACK], BF16, name="wa_sb")
         u_sb = keep.tile([P, PACK], BF16, name="u_sb")
         t_sb = keep.tile([P, PACK], BF16, name="t_sb")
         wf_w = keep.tile([P, 2, 2 * S], U8, name="wf_w", align_bytes=64)
         wv_w = keep.tile([P, 2, 2 * V], U8, name="wv_w", align_bytes=64)
         rnd_sb = keep.tile([P, PACK, S], BF16, name="rnd_sb")
 
-        for k in range(PACK):
-            load_x(0, k, 1)
-        nc.scalar.dma_start(out=wa_sb[:], in_=wa.rearrange("(g p t) -> p g t", g=2, t=PACK))
-        for q in range(4):
-            nc.scalar.dma_start(
-                out=wf_s[32 * q : 32 * q + 4, :, :].bitcast(I32),
-                in_=wf_scales[:, 4 * q : 4 * q + 4, :].rearrange("g r n -> r g n").bitcast(I32),
-            )
-        for q in range(4):
-            nc.scalar.dma_start(
-                out=wv_s[32 * q : 32 * q + 4, :, :].bitcast(I32),
-                in_=wv_scales[:, 4 * q : 4 * q + 4, :].rearrange("g r n -> r g n").bitcast(I32),
-            )
-        nc.scalar.dma_start(out=t_sb[:], in_=t.rearrange("(p t) -> p t", t=PACK))
-        nc.scalar.dma_start(out=u_sb[:], in_=u.rearrange("(p t) -> p t", t=PACK))
-        nc.sync.dma_start(out=wf_w[:].bitcast(I32), in_=wf_words.rearrange("g p n -> p g n").bitcast(I32))
+        def load_scales(queue, plane, scales):
+            for q in range(4):
+                queue.dma_start(
+                    out=plane[32 * q : 32 * q + 4, :, :].bitcast(I32),
+                    in_=scales[:, 4 * q : 4 * q + 4, :].rearrange("g r n -> r g n").bitcast(I32),
+                )
+
+        load_x(0, 0, 1)
+        load_x(0, 1, 1)
+        load_x(0, 2, 2)
+        load_scales(nc.scalar, wv_s, wv_scales)
+        load_scales(nc.gpsimd, wf_s, wf_scales)
+        nc.sync.dma_start(
+            out=wa_sb[:, 0 : 2 * PACK].rearrange("p (g t) -> p g t", g=2), in_=wa.rearrange("(g p t) -> p g t", g=2, t=PACK)
+        )
         nc.sync.dma_start(out=wv_w[:].bitcast(I32), in_=wv_words.rearrange("g p n -> p g n").bitcast(I32))
+        nc.sync.dma_start(out=t_sb[:], in_=t.rearrange("(p t) -> p t", t=PACK))
+        nc.sync.dma_start(out=wf_w[:].bitcast(I32), in_=wf_words.rearrange("g p n -> p g n").bitcast(I32))
         nc.sync.dma_start(out=rnd_sb[:], in_=rnd.rearrange("(m t) j -> m t j", t=PACK))
+        nc.sync.dma_start(out=u_sb[:], in_=u.rearrange("(p t) -> p t", t=PACK))
         for b in range(1, B):
             load_x(b, 0, 2)
             load_x(b, 2, 2)
 
         warm = keep.tile([P, 1], F32, name="warm")
         nc.scalar.activation(out=warm[:], in_=ident[:, 0:1], func=ACT.Exp)
+        rnd_p = keep.tile([P, PACK, S], BF16, name="rnd_p")
+        t32 = keep.tile([P, PACK], F32, name="t32")
+        nc.gpsimd.tensor_scalar(out=t32[:], in0=t_sb[:], scalar1=1.0, scalar2=0.0, op0=ALU.mult, op1=ALU.add)
         u512 = keep.tile([P, PACK], F32, name="u512")
-        nc.gpsimd.tensor_scalar(out=u512[:], in0=u_sb[:], scalar1=float(S), scalar2=0.0, op0=ALU.mult, op1=ALU.add)
+
+        def rnd_permute(k):
+            nc.scalar.copy(
+                out=rnd_p[:, k, :].rearrange("q (j p) -> q j p", j=PACK),
+                in_=rnd_sb[:, k, :].rearrange("q (p j) -> q j p", j=PACK),
+            )
 
         xg, xq, xs = {}, {}, {}
-        rho, nsg, zneg = {}, {}, {}
+        rho, nsg, zneg, rho_all, vrow = {}, {}, {}, {}, {}
         banks = {}
         y, nl, nm, e, esum, rinv, w = {}, {}, {}, {}, {}, {}, {}
         cg, cq, cs = {}, {}, {}
@@ -142,42 +194,51 @@ def tile_tokengatedmixtureofsynthesizers_x2_kernel(
             xs[n] = work.tile([P, 2 * P], U8, name="xs", bufs=12, align_bytes=64)
             nc.vector.quantize_mx(out=xq[n][:].bitcast(FP8X4), scales=xs[n][:], in_=xg[n][:])
 
-        def gate_mm(b):
+        def group(n):
+            return [n] if n < PACK else list(range(n - n % PACK, n - n % PACK + PACK))
+
+        def gate_mm(n):
             bk = next_bank()
-            banks["g", b] = bk
-            for k in range(PACK):
-                xv = xg[PACK * b + k][:].rearrange("p (g m t) -> p g t m", g=2, t=PACK)
+            banks["g", n] = bk
+            for k, m in enumerate(group(n)):
+                xv = xg[m][:].rearrange("p (g m t) -> p g t m", g=2, t=PACK)
                 for g in range(2):
                     for j in range(PACK):
                         nc.tensor.matmul(
-                            out=bk[:, k : k + 1],
+                            out=bk[:, k * GATE_N : (k + 1) * GATE_N],
                             lhsT=xv[:, g, j, :],
-                            rhs=wa_sb[:, g, j : j + 1],
+                            rhs=wa_sb[:, PACK * g + j : PACK * g + j + GATE_N],
                             start=(g == 0 and j == 0),
                             stop=(g == 1 and j == PACK - 1),
                         )
 
-        def gate_clamp(b):
-            zneg[b] = work.tile([P, PACK], F32, name="zneg", bufs=2)
-            nc.vector.tensor_scalar(
-                out=zneg[b][:], in0=banks["g", b][:, 0:PACK], scalar1=-1.0, scalar2=GATE_CLAMP, op0=ALU.mult, op1=ALU.min
+        def gate_exp(n):
+            k = len(group(n))
+            zneg[n] = work.tile([P, k], F32, name="zexp", bufs=3)
+            nc.scalar.activation(out=zneg[n][:], in_=banks["g", n][:, 0 : k * GATE_N : GATE_N], func=ACT.Exp, scale=-1.0)
+
+        def gate_clamp(n):
+            r = work.tile([P, len(group(n))], F32, name="rho", bufs=5)
+            nc.gpsimd.tensor_scalar(out=r[:], in0=zneg[n][:], scalar1=RHO_MAX, scalar2=-1.0, op0=ALU.min, op1=ALU.mult)
+            rho_all[n] = r
+            for k, m in enumerate(group(n)):
+                rho[m] = r[:, k : k + 1]
+
+        def gate_den(n):
+            zneg[n] = work.tile([P, len(group(n))], F32, name="gden", bufs=3)
+            nc.gpsimd.tensor_scalar(
+                out=zneg[n][:], in0=rho_all[n][:], scalar1=-0.5, scalar2=0.5, op0=ALU.mult, op1=ALU.add
             )
 
-        def gate_exp(b):
-            rho[b] = work.tile([P, PACK], F32, name="rho", bufs=2)
-            nc.scalar.activation(out=rho[b][:], in_=zneg[b][:], func=ACT.Exp)
-
-        def gate_den(b):
-            zneg[b] = work.tile([P, PACK], F32, name="gden", bufs=2)
-            nc.vector.tensor_scalar(
-                out=zneg[b][:], in0=rho[b][:], scalar1=-0.5, scalar2=-0.5, op0=ALU.mult, op1=ALU.add
-            )
-
-        def gate_recip(b):
-            nsg[b] = work.tile([P, PACK], F32, name="nsg", bufs=2)
-            nc.vector.reciprocal(out=nsg[b][:], in_=zneg[b][:])
+        def gate_recip(n):
+            r = work.tile([P, len(group(n))], F32, name="nsg", bufs=5)
+            nc.vector.reciprocal(out=r[:], in_=zneg[n][:])
+            for k, m in enumerate(group(n)):
+                nsg[m] = r[:, k : k + 1]
 
         def f_mm(n):
+            if n < PACK:
+                rnd_permute(n)
             bk = next_bank()
             banks["f", n] = bk
             for g in range(2):
@@ -196,11 +257,11 @@ def tile_tokengatedmixtureofsynthesizers_x2_kernel(
             y[n] = work.tile([P, S], F32, name="y", bufs=3)
             nc.vector.scalar_tensor_tensor(
                 out=y[n][:].rearrange("q (j p) -> q j p", j=PACK),
-                in0=rnd_sb[:, k, :].rearrange("q (p j) -> q j p", j=PACK),
-                scalar=rho[b][:, k : k + 1],
+                in0=rnd_p[:, k, :].rearrange("q (j p) -> q j p", j=PACK),
+                scalar=rho[n],
                 in1=banks["f", n][:].rearrange("q (p j) -> q j p", j=PACK),
                 op0=ALU.mult,
-                op1=ALU.add,
+                op1=ALU.subtract,
             )
 
         def row_max(n):
@@ -208,7 +269,7 @@ def tile_tokengatedmixtureofsynthesizers_x2_kernel(
             nl[n] = work.tile([P, S], F32, name="nl", bufs=3)
             nm[n] = work.tile([P, 1], F32, name="nm", bufs=3)
             nc.vector.tensor_scalar(
-                out=nl[n][:], in0=y[n][:], scalar1=nsg[b][:, k : k + 1], scalar2=None,
+                out=nl[n][:], in0=y[n][:], scalar1=nsg[n], scalar2=None,
                 op0=ALU.mult, op1=ALU.min, accum_out=nm[n][:],
             )
 
@@ -222,6 +283,8 @@ def tile_tokengatedmixtureofsynthesizers_x2_kernel(
             nc.vector.reciprocal(out=rinv[n][:], in_=esum[n][:])
 
         def normalise(n):
+            if n == 0:
+                nc.gpsimd.tensor_scalar(out=u512[:], in0=u_sb[:], scalar1=float(S), scalar2=0.0, op0=ALU.mult, op1=ALU.add)
             w[n] = work.tile([P, S], F32, name="w", bufs=3)
             if ENGINES["w"][n] == "G":
                 nc.gpsimd.tensor_scalar(
@@ -254,31 +317,69 @@ def tile_tokengatedmixtureofsynthesizers_x2_kernel(
             cs[n] = work.tile([P, P], U8, name="cs", bufs=6, align_bytes=64)
             nc.vector.quantize_mx(out=cq[n][:].bitcast(FP8X4), scales=cs[n][:], in_=cg[n][:])
 
-        def h_mm(b, k):
+        def h_narrow(n):
+            b, k = divmod(n, PACK)
             bk = next_bank()
-            banks["h", b, k] = bk
+            banks["h0", n] = bk
             for j in range(PACK):
-                n = PACK * b + j
+                m = PACK * b + j
                 for g in range(2):
                     nc.tensor.matmul_mx(
                         out=bk[:, j * P : (j + 1) * P],
-                        lhsT=xq[n][:, g * P : (g + 1) * P].bitcast(FP8X4),
-                        lhsT_scale=xs[n][:, g * P : (g + 1) * P],
+                        lhsT=xq[m][:, g * P : (g + 1) * P].bitcast(FP8X4),
+                        lhsT_scale=xs[m][:, g * P : (g + 1) * P],
                         rhs=wv_w[:, g, 2 * P * k : 2 * P * (k + 1)].bitcast(FP4X4),
                         rhs_scale=wv_s[:, g, P * k : P * (k + 1)],
                         start=(g == 0),
                         stop=(g == 1),
                     )
 
-        def v_form(b, k):
-            half, kk = divmod(k, PACK)
+        def h_wide(n):
+            bk = next_bank()
+            banks["h1", n] = bk
+            for g in range(2):
+                nc.tensor.matmul_mx(
+                    out=bk[:],
+                    lhsT=xq[n][:, g * P : (g + 1) * P].bitcast(FP8X4),
+                    lhsT_scale=xs[n][:, g * P : (g + 1) * P],
+                    rhs=wv_w[:, g, 2 * KP : 4 * KP].bitcast(FP4X4),
+                    rhs_scale=wv_s[:, g, KP : 2 * KP],
+                    start=(g == 0),
+                    stop=(g == 1),
+                )
+
+        def v_tile(b, half):
             if (b, half) not in vg:
-                vg[b, half] = work.tile([P, KP * PACK], BF16, name="vg", bufs=3, align_bytes=64)
+                vg[b, half] = work.tile([P, KP * PACK], BF16, name="vg", bufs=4, align_bytes=64)
+            return vg[b, half]
+
+        def v_narrow(n):
+            b, k = divmod(n, PACK)
             nc.vector.tensor_tensor(
-                out=vg[b, half][:, kk * KP : (kk + 1) * KP].rearrange("p (m j) -> p m j", j=PACK),
-                in0=banks["h", b, k][:].rearrange("p (j m) -> p m j", j=PACK),
+                out=v_tile(b, 0)[:, k * KP : (k + 1) * KP].rearrange("p (m j) -> p m j", j=PACK),
+                in0=banks["h0", n][:].rearrange("p (j m) -> p m j", j=PACK),
                 in1=t_sb[:].unsqueeze(1).broadcast_to([P, P, PACK]),
                 op=ALU.mult,
+            )
+
+        def v_wide(n):
+            b, k = divmod(n, PACK)
+            if b not in vrow:
+                vrow[b] = work.tile([P, PACK, KP], BF16, name="vrow", bufs=2)
+            if ENGINES["v1"][n] == "D":
+                nc.vector.tensor_scalar(
+                    out=vrow[b][:, k, :], in0=banks["h1", n][:], scalar1=t32[:, k : k + 1], scalar2=None, op0=ALU.mult
+                )
+            else:
+                nc.scalar.activation(out=vrow[b][:, k, :], in_=banks["h1", n][:], func=ACT.Copy, scale=t32[:, k : k + 1])
+
+        def v_interleave(n):
+            b, k = divmod(n, PACK)
+            run = 1 if ENGINES["il"][n] == "G" else PACK
+            copy_on(
+                "il", n,
+                out=v_tile(b, 1)[:, k * KP : (k + 1) * KP].rearrange("p (c i j) -> p c j i", i=run, j=PACK),
+                in_=vrow[b][:, :, k * P : (k + 1) * P].rearrange("p j (c i) -> p c j i", i=run),
             )
 
         def v_quant(b, half):
@@ -363,30 +464,31 @@ def tile_tokengatedmixtureofsynthesizers_x2_kernel(
         every_tile = {
             "X": x_transpose, "xc": x_copy, "xq": x_quant, "F": f_mm, "y": mix, "mx": row_max, "ex": exp_sum,
             "rc": sum_recip, "w": normalise, "C": c_transpose, "cf": c_form, "cq": c_quant, "st": o_store,
-            "H0": lambda n: h_mm(n // PACK, 2 * (n % PACK)), "H1": lambda n: h_mm(n // PACK, 2 * (n % PACK) + 1),
-            "v0": lambda n: v_form(n // PACK, 2 * (n % PACK)), "v1": lambda n: v_form(n // PACK, 2 * (n % PACK) + 1),
+            "H0": h_narrow, "H1": h_wide, "v0": v_narrow, "v1": v_wide, "il": v_interleave,
             "O0": lambda n: o_mm(n, 0), "O1": lambda n: o_mm(n, 1),
             "e0": lambda n: o_evac(n, 0), "e1": lambda n: o_evac(n, 1),
             "k0": lambda n: o_cast(n, 0), "k1": lambda n: o_cast(n, 1),
         }
         every_pair = {
-            "vq": lambda n: v_quant(n // PACK, (n % PACK) // 2),
             "T0": lambda n: o_transpose(n // 2, 0), "T1": lambda n: o_transpose(n // 2, 1),
             "og0": lambda n: o_gather(n // 2, 0), "og1": lambda n: o_gather(n // 2, 1),
         }
         every_batch = {
-            "G": gate_mm, "gc": gate_clamp, "ge": gate_exp, "gd": gate_den, "gr": gate_recip,
+            "vq0": lambda b: v_quant(b, 0), "vq1": lambda b: v_quant(b, 1),
             "oq0": lambda b: o_quant(b, 0), "oq1": lambda b: o_quant(b, 1),
             "ps0": lambda b: plane_store(b, 0), "ps1": lambda b: plane_store(b, 1),
         }
-        for s in range(NT + max(lag for name, lag in STEP)):
-            for name, lag in STEP:
-                n = s - lag
-                if not 0 <= n < NT:
-                    continue
-                if name in every_tile:
-                    every_tile[name](n)
-                elif name in every_pair and n % 2 == 1:
-                    every_pair[name](n)
-                elif name in every_batch and n % PACK == PACK - 1:
-                    every_batch[name](n // PACK)
+        every_group = {"G": gate_mm, "gc": gate_clamp, "ge": gate_exp, "gd": gate_den, "gr": gate_recip}
+        for s in range(NT + max(max(lags) for name, lags in STEP)):
+            for name, lags in STEP:
+                for n in range(NT):
+                    if n + lags[n // PACK] != s:
+                        continue
+                    if name in every_tile:
+                        every_tile[name](n)
+                    elif name in every_pair and n % 2 == 1:
+                        every_pair[name](n)
+                    elif name in every_batch and n % PACK == PACK - 1:
+                        every_batch[name](n // PACK)
+                    elif name in every_group and n == group(n)[-1]:
+                        every_group[name](n)

import math
from contextlib import ExitStack

import concourse.mybir as mybir
from concourse.masks import make_identity

B, S, D, V = 4, 512, 1024, 1024
FLOPS = 2 * B * S * (D * S + D * V + S * V)

F32 = mybir.dt.float32
BF16 = mybir.dt.bfloat16
U32 = mybir.dt.uint32
I32 = mybir.dt.int32
U8 = mybir.dt.uint8
FP8X4 = mybir.dt.float8_e4m3fn_x4
FP4X4 = mybir.dt.float4_e2m1fn_x4
ALU = mybir.AluOpType
ACT = mybir.ActivationFunctionType

P = 128
PACK = 4
KP = 512
NT = B * PACK
BANKS = 8
RHO_MAX = 2.0**64
GATE_N = 64
STEP = [
    ("X", (0, 0, 0, 0)),
    ("v1", (3, 3, 3, 3)),
    ("C", (8, 8, 8, 8)),
    ("og1", (13, 13, 13, 13)),
    ("T0", (11, 11, 11, 11)),
    ("cf", (8, 8, 8, 8)),
    ("oq0", (13, 13, 13, 13)),
    ("xc", (0, 0, 0, 0)),
    ("il", (6, 6, 6, 6)),
    ("xq", (0, 0, 0, 0)),
    ("ps0", (14, 14, 14, 14)),
    ("G", (1, 1, 1, 1)),
    ("k0", (10, 10, 10, 10)),
    ("vq1", (6, 6, 6, 6)),
    ("O1", (10, 10, 10, 10)),
    ("k1", (11, 11, 11, 11)),
    ("O0", (9, 9, 9, 9)),
    ("og0", (11, 11, 11, 11)),
    ("ge", (1, 1, 1, 1)),
    ("F", (4, 4, 4, 4)),
    ("vq0", (5, 5, 5, 5)),
    ("oq1", (15, 15, 15, 15)),
    ("st", (11, 11, 11, 11)),
    ("gc", (1, 1, 1, 1)),
    ("rc", (6, 6, 6, 6)),
    ("cq", (8, 8, 8, 8)),
    ("y", (4, 4, 4, 4)),
    ("H0", (4, 4, 4, 4)),
    ("gd", (1, 1, 1, 1)),
    ("e1", (10, 10, 10, 10)),
    ("H1", (2, 2, 2, 2)),
    ("gr", (1, 1, 1, 1)),
    ("w", (6, 6, 6, 6)),
    ("v0", (4, 4, 4, 4)),
    ("e0", (9, 9, 9, 9)),
    ("ps1", (15, 15, 15, 15)),
    ("mx", (4, 4, 4, 4)),
    ("ex", (5, 5, 5, 5)),
    ("T1", (12, 12, 12, 12))
]
ENGINES = {
    "w": "GGGGGGGGGGGGGGGG",
    "xc": "AAAAAAAAAAAAAAAA",
    "v1": "AAAAAAAAAAAAAAAA",
    "il": "AAGGAAAAAAAAAAAA",
    "e0": "AAAAAAAAAAAAAAAA",
    "e1": "AAAAAAAAAAAAAAAA",
    "k0": "GGGGGGGGGGGDADDD",
    "k1": "GGGGGGGGGGDDDDDD",
    "og0": "AAAAAAAAAAAADDAA",
    "og1": "AAAAAAAAAAAAAAAA"
}


def tile_tokengatedmixtureofsynthesizers_x2_kernel(
    tc, x, wf_words, wf_scales, rnd, wa, wv_words, wv_scales, u, t, out_0, out_1, out_2
):
    nc = tc.nc
    with ExitStack() as ctx:
        keep = ctx.enter_context(tc.tile_pool(name="keep", bufs=1))
        work = ctx.enter_context(tc.tile_pool(name="work", bufs=3))
        psum = ctx.enter_context(tc.psum_pool(name="psum", bufs=1))
        ctx.enter_context(tc.manual_schedule())

        def copy_on(kind, n, out, in_):
            if ENGINES[kind][n] == "D":
                nc.vector.tensor_copy(out=out, in_=in_)
            elif ENGINES[kind][n] == "G":
                nc.gpsimd.tensor_scalar(out=out, in0=in_, scalar1=1.0, scalar2=0.0, op0=ALU.mult, op1=ALU.add)
            else:
                nc.scalar.copy(out=out, in_=in_)

        bank_count = [0]

        def next_bank():
            k = bank_count[0] % BANKS
            bank_count[0] += 1
            return psum.tile([P, KP], F32, name="bank%d" % k)

        ident = keep.tile([P, P], F32, name="ident")
        make_identity(nc, ident[:])
        wa_sb = keep.tile([P, 2 * PACK + GATE_N], BF16, name="wa_sb")
        nc.vector.memset(wa_sb[:].bitcast(I32), 0)
        wf_s = keep.tile([P, 2, S], U8, name="wf_s", align_bytes=64)
        wv_s = keep.tile([P, 2, V], U8, name="wv_s", align_bytes=64)
        nc.vector.memset(wv_s[:].rearrange("p g n -> p (g n)").bitcast(I32), 0)
        nc.vector.memset(wf_s[:].rearrange("p g n -> p (g n)").bitcast(I32), 0)

        x_sb = {}

        def load_x(b, t0, n):
            xt = keep.tile([P, n, D], BF16, name="x_%d_%d" % (b, t0))
            nc.sync.dma_start(out=xt[:], in_=x[b].rearrange("(m t) d -> m t d", t=PACK)[:, t0 : t0 + n, :])
            for k in range(n):
                x_sb[PACK * b + t0 + k] = xt[:, k, :]

        u_sb = keep.tile([P, PACK], BF16, name="u_sb")
        t_sb = keep.tile([P, PACK], BF16, name="t_sb")
        wf_w = keep.tile([P, 2, 2 * S], U8, name="wf_w", align_bytes=64)
        wv_w = keep.tile([P, 2, 2 * V], U8, name="wv_w", align_bytes=64)
        rnd_sb = keep.tile([P, PACK, S], BF16, name="rnd_sb")

        def load_scales(queue, plane, scales):
            for q in range(4):
                queue.dma_start(
                    out=plane[32 * q : 32 * q + 4, :, :].bitcast(I32),
                    in_=scales[:, 4 * q : 4 * q + 4, :].rearrange("g r n -> r g n").bitcast(I32),
                )

        load_x(0, 0, 1)
        load_x(0, 1, 1)
        load_x(0, 2, 2)
        load_scales(nc.scalar, wv_s, wv_scales)
        load_scales(nc.gpsimd, wf_s, wf_scales)
        nc.sync.dma_start(
            out=wa_sb[:, 0 : 2 * PACK].rearrange("p (g t) -> p g t", g=2), in_=wa.rearrange("(g p t) -> p g t", g=2, t=PACK)
        )
        nc.sync.dma_start(out=wv_w[:].bitcast(I32), in_=wv_words.rearrange("g p n -> p g n").bitcast(I32))
        nc.sync.dma_start(out=t_sb[:], in_=t.rearrange("(p t) -> p t", t=PACK))
        nc.sync.dma_start(out=wf_w[:].bitcast(I32), in_=wf_words.rearrange("g p n -> p g n").bitcast(I32))
        nc.sync.dma_start(out=rnd_sb[:], in_=rnd.rearrange("(m t) j -> m t j", t=PACK))
        nc.sync.dma_start(out=u_sb[:], in_=u.rearrange("(p t) -> p t", t=PACK))
        for b in range(1, B):
            load_x(b, 0, 2)
            load_x(b, 2, 2)

        warm = keep.tile([P, 1], F32, name="warm")
        nc.scalar.activation(out=warm[:], in_=ident[:, 0:1], func=ACT.Exp)
        rnd_p = keep.tile([P, PACK, S], BF16, name="rnd_p")
        t32 = keep.tile([P, PACK], F32, name="t32")
        nc.gpsimd.tensor_scalar(out=t32[:], in0=t_sb[:], scalar1=1.0, scalar2=0.0, op0=ALU.mult, op1=ALU.add)
        u512 = keep.tile([P, PACK], F32, name="u512")

        def rnd_permute(k):
            nc.scalar.copy(
                out=rnd_p[:, k, :].rearrange("q (j p) -> q j p", j=PACK),
                in_=rnd_sb[:, k, :].rearrange("q (p j) -> q j p", j=PACK),
            )

        xg, xq, xs = {}, {}, {}
        rho, nsg, zneg, rho_all, vrow = {}, {}, {}, {}, {}
        banks = {}
        y, nl, nm, e, esum, rinv, w = {}, {}, {}, {}, {}, {}, {}
        cg, cq, cs = {}, {}, {}
        vg, vq, vs = {}, {}, {}
        o32, ob, og, oq, osc = {}, {}, {}, {}, {}

        def x_transpose(n):
            bk = next_bank()
            banks["x", n] = bk
            words = x_sb[n].bitcast(F32)
            for g in range(2):
                for h in range(2):
                    c0 = (2 * g + h) * P
                    nc.tensor.transpose(bk[:, c0 : c0 + P], words[:, 256 * g + h : 256 * (g + 1) : 2], ident[:])

        def x_copy(n):
            xg[n] = work.tile([P, 2 * P * PACK], BF16, name="xg", bufs=8, align_bytes=64)
            copy_on(
                "xc", n,
                out=xg[n][:].bitcast(F32).rearrange("p (g m h) -> p g m h", g=2, h=2),
                in_=banks["x", n][:].rearrange("p (g h m) -> p g m h", g=2, h=2),
            )

        def x_quant(n):
            xq[n] = work.tile([P, 2 * P], U32, name="xq", bufs=12, align_bytes=64)
            xs[n] = work.tile([P, 2 * P], U8, name="xs", bufs=12, align_bytes=64)
            nc.vector.quantize_mx(out=xq[n][:].bitcast(FP8X4), scales=xs[n][:], in_=xg[n][:])

        def group(n):
            return [n] if n < PACK else list(range(n - n % PACK, n - n % PACK + PACK))

        def gate_mm(n):
            bk = next_bank()
            banks["g", n] = bk
            for k, m in enumerate(group(n)):
                xv = xg[m][:].rearrange("p (g m t) -> p g t m", g=2, t=PACK)
                for g in range(2):
                    for j in range(PACK):
                        nc.tensor.matmul(
                            out=bk[:, k * GATE_N : (k + 1) * GATE_N],
                            lhsT=xv[:, g, j, :],
                            rhs=wa_sb[:, PACK * g + j : PACK * g + j + GATE_N],
                            start=(g == 0 and j == 0),
                            stop=(g == 1 and j == PACK - 1),
                        )

        def gate_exp(n):
            k = len(group(n))
            zneg[n] = work.tile([P, k], F32, name="zexp", bufs=3)
            nc.scalar.activation(out=zneg[n][:], in_=banks["g", n][:, 0 : k * GATE_N : GATE_N], func=ACT.Exp, scale=-1.0)

        def gate_clamp(n):
            r = work.tile([P, len(group(n))], F32, name="rho", bufs=5)
            nc.gpsimd.tensor_scalar(out=r[:], in0=zneg[n][:], scalar1=RHO_MAX, scalar2=-1.0, op0=ALU.min, op1=ALU.mult)
            rho_all[n] = r
            for k, m in enumerate(group(n)):
                rho[m] = r[:, k : k + 1]

        def gate_den(n):
            zneg[n] = work.tile([P, len(group(n))], F32, name="gden", bufs=3)
            nc.gpsimd.tensor_scalar(
                out=zneg[n][:], in0=rho_all[n][:], scalar1=-0.5, scalar2=0.5, op0=ALU.mult, op1=ALU.add
            )

        def gate_recip(n):
            r = work.tile([P, len(group(n))], F32, name="nsg", bufs=5)
            nc.vector.reciprocal(out=r[:], in_=zneg[n][:])
            for k, m in enumerate(group(n)):
                nsg[m] = r[:, k : k + 1]

        def f_mm(n):
            if n < PACK:
                rnd_permute(n)
            bk = next_bank()
            banks["f", n] = bk
            for g in range(2):
                nc.tensor.matmul_mx(
                    out=bk[:],
                    lhsT=xq[n][:, g * P : (g + 1) * P].bitcast(FP8X4),
                    lhsT_scale=xs[n][:, g * P : (g + 1) * P],
                    rhs=wf_w[:, g, :].bitcast(FP4X4),
                    rhs_scale=wf_s[:, g, :],
                    start=(g == 0),
                    stop=(g == 1),
                )

        def mix(n):
            b, k = divmod(n, PACK)
            y[n] = work.tile([P, S], F32, name="y", bufs=3)
            nc.vector.scalar_tensor_tensor(
                out=y[n][:].rearrange("q (j p) -> q j p", j=PACK),
                in0=rnd_p[:, k, :].rearrange("q (j p) -> q j p", j=PACK),
                scalar=rho[n],
                in1=banks["f", n][:].rearrange("q (p j) -> q j p", j=PACK),
                op0=ALU.mult,
                op1=ALU.subtract,
            )

        def row_max(n):
            b, k = divmod(n, PACK)
            nl[n] = work.tile([P, S], F32, name="nl", bufs=3)
            nm[n] = work.tile([P, 1], F32, name="nm", bufs=3)
            nc.vector.tensor_scalar(
                out=nl[n][:], in0=y[n][:], scalar1=nsg[n], scalar2=None,
                op0=ALU.mult, op1=ALU.min, accum_out=nm[n][:],
            )

        def exp_sum(n):
            e[n] = work.tile([P, S], F32, name="e", bufs=3)
            esum[n] = work.tile([P, 1], F32, name="esum", bufs=3)
            nc.scalar.activation(out=e[n][:], in_=nl[n][:], func=ACT.Exp, bias=nm[n][:], scale=-1.0, accum_out=esum[n][:])

        def sum_recip(n):
            rinv[n] = work.tile([P, 1], F32, name="rinv", bufs=3)
            nc.vector.reciprocal(out=rinv[n][:], in_=esum[n][:])

        def normalise(n):
            if n == 0:
                nc.gpsimd.tensor_scalar(out=u512[:], in0=u_sb[:], scalar1=float(S), scalar2=0.0, op0=ALU.mult, op1=ALU.add)
            w[n] = work.tile([P, S], F32, name="w", bufs=3)
            if ENGINES["w"][n] == "G":
                nc.gpsimd.tensor_scalar(
                    out=w[n][:], in0=e[n][:], scalar1=rinv[n][:], scalar2=0.0, op0=ALU.mult, op1=ALU.add
                )
            elif ENGINES["w"][n] == "D":
                nc.vector.tensor_scalar(out=w[n][:], in0=e[n][:], scalar1=rinv[n][:], scalar2=None, op0=ALU.mult)
            else:
                nc.scalar.activation(out=w[n][:], in_=e[n][:], func=ACT.Copy, scale=rinv[n][:])

        def c_transpose(n):
            bk = next_bank()
            banks["c", n] = bk
            for j in range(PACK):
                nc.tensor.transpose(bk[:, j * P : (j + 1) * P], w[n][:, j * P : (j + 1) * P], ident[:])

        def c_form(n):
            cg[n] = work.tile([P, P * PACK], BF16, name="cg", bufs=3, align_bytes=64)
            nc.vector.scalar_tensor_tensor(
                out=cg[n][:].rearrange("p (i j) -> p i j", j=PACK),
                in0=banks["c", n][:].rearrange("p (j i) -> p i j", j=PACK),
                scalar=1.0 / S,
                in1=u512[:].unsqueeze(1).broadcast_to([P, P, PACK]),
                op0=ALU.subtract,
                op1=ALU.mult,
            )

        def c_quant(n):
            cq[n] = work.tile([P, P], U32, name="cq", bufs=6, align_bytes=64)
            cs[n] = work.tile([P, P], U8, name="cs", bufs=6, align_bytes=64)
            nc.vector.quantize_mx(out=cq[n][:].bitcast(FP8X4), scales=cs[n][:], in_=cg[n][:])

        def h_narrow(n):
            b, k = divmod(n, PACK)
            bk = next_bank()
            banks["h0", n] = bk
            for j in range(PACK):
                m = PACK * b + j
                for g in range(2):
                    nc.tensor.matmul_mx(
                        out=bk[:, j * P : (j + 1) * P],
                        lhsT=xq[m][:, g * P : (g + 1) * P].bitcast(FP8X4),
                        lhsT_scale=xs[m][:, g * P : (g + 1) * P],
                        rhs=wv_w[:, g, 2 * P * k : 2 * P * (k + 1)].bitcast(FP4X4),
                        rhs_scale=wv_s[:, g, P * k : P * (k + 1)],
                        start=(g == 0),
                        stop=(g == 1),
                    )

        def h_wide(n):
            bk = next_bank()
            banks["h1", n] = bk
            for g in range(2):
                nc.tensor.matmul_mx(
                    out=bk[:],
                    lhsT=xq[n][:, g * P : (g + 1) * P].bitcast(FP8X4),
                    lhsT_scale=xs[n][:, g * P : (g + 1) * P],
                    rhs=wv_w[:, g, 2 * KP : 4 * KP].bitcast(FP4X4),
                    rhs_scale=wv_s[:, g, KP : 2 * KP],
                    start=(g == 0),
                    stop=(g == 1),
                )

        def v_tile(b, half):
            if (b, half) not in vg:
                vg[b, half] = work.tile([P, KP * PACK], BF16, name="vg", bufs=4, align_bytes=64)
            return vg[b, half]

        def v_narrow(n):
            b, k = divmod(n, PACK)
            nc.vector.tensor_tensor(
                out=v_tile(b, 0)[:, k * KP : (k + 1) * KP].rearrange("p (m j) -> p m j", j=PACK),
                in0=banks["h0", n][:].rearrange("p (j m) -> p m j", j=PACK),
                in1=t_sb[:].unsqueeze(1).broadcast_to([P, P, PACK]),
                op=ALU.mult,
            )

        def v_wide(n):
            b, k = divmod(n, PACK)
            if b not in vrow:
                vrow[b] = work.tile([P, PACK, KP], BF16, name="vrow", bufs=2)
            if ENGINES["v1"][n] == "D":
                nc.vector.tensor_scalar(
                    out=vrow[b][:, k, :], in0=banks["h1", n][:], scalar1=t32[:, k : k + 1], scalar2=None, op0=ALU.mult
                )
            else:
                nc.scalar.activation(out=vrow[b][:, k, :], in_=banks["h1", n][:], func=ACT.Copy, scale=t32[:, k : k + 1])

        def v_interleave(n):
            b, k = divmod(n, PACK)
            run = 1 if ENGINES["il"][n] == "G" else PACK
            copy_on(
                "il", n,
                out=v_tile(b, 1)[:, k * KP : (k + 1) * KP].rearrange("p (c i j) -> p c j i", i=run, j=PACK),
                in_=vrow[b][:, :, k * P : (k + 1) * P].rearrange("p j (c i) -> p c j i", i=run),
            )

        def v_quant(b, half):
            vq[b, half] = work.tile([P, KP], U32, name="vq", bufs=5, align_bytes=64)
            vs[b, half] = work.tile([P, KP], U8, name="vs", bufs=5, align_bytes=64)
            nc.vector.quantize_mx(out=vq[b, half][:].bitcast(FP8X4), scales=vs[b, half][:], in_=vg[b, half][:])

        def o_mm(n, half):
            b = n // PACK
            bk = next_bank()
            banks["o", n, half] = bk
            nc.tensor.matmul_mx(
                out=bk[:],
                lhsT=cq[n][:].bitcast(FP8X4),
                lhsT_scale=cs[n][:],
                rhs=vq[b, half][:].bitcast(FP8X4),
                rhs_scale=vs[b, half][:],
                start=True,
                stop=True,
            )

        def o_evac(n, half):
            if n not in o32:
                o32[n] = work.tile([P, V], F32, name="o32", bufs=6)
            dst = o32[n][:, half * KP : (half + 1) * KP]
            if ENGINES["e%d" % half][n] == "D":
                nc.vector.tensor_scalar(
                    out=dst, in0=banks["o", n, half][:], scalar1=1.0 / math.sqrt(S), scalar2=None, op0=ALU.mult
                )
            else:
                nc.scalar.activation(out=dst, in_=banks["o", n, half][:], func=ACT.Copy, scale=1.0 / math.sqrt(S))

        def o_store(n):
            b, k = divmod(n, PACK)
            nc.sync.dma_start(out=out_0[b].rearrange("(m t) v -> m t v", t=PACK)[:, k, :], in_=o32[n][:])

        def o_cast(n, half):
            ob[n, half] = work.tile([P, KP], BF16, name="ob", bufs=8)
            copy_on(
                "k%d" % half, n,
                out=ob[n, half][:].rearrange("q (h p e) -> q h p e", h=2, e=2),
                in_=o32[n][:, half * KP : (half + 1) * KP].rearrange("q (p h e) -> q h p e", h=2, e=2),
            )

        def o_transpose(pair, g):
            bk = next_bank()
            banks["t", pair, g] = bk
            for a in range(2):
                words = ob[2 * pair + a, g][:].bitcast(F32)
                for h in range(2):
                    c0 = (2 * a + h) * P
                    nc.tensor.transpose(bk[:, c0 : c0 + P], words[:, h * P : (h + 1) * P], ident[:])

        def o_gather(pair, g):
            b, pp = divmod(pair, 2)
            if pp == 0:
                og[b, g] = work.tile([P, S * PACK], BF16, name="og", bufs=4, align_bytes=64)
            copy_on(
                "og%d" % g, 2 * pair + 1,
                out=og[b, g][:].bitcast(F32).rearrange("p (m c) -> p m c", c=8)[:, :, 4 * pp : 4 * pp + 4],
                in_=banks["t", pair, g][:].rearrange("p (c m) -> p m c", c=4),
            )

        def o_quant(b, g):
            oq[b, g] = work.tile([P, S], U32, name="oq", bufs=3, align_bytes=64)
            if b not in osc:
                osc[b] = work.tile([P, 2, S], U8, name="osc", bufs=2, align_bytes=64)
            nc.vector.quantize_mx(out=oq[b, g][:].bitcast(FP8X4), scales=osc[b][:, g, :], in_=og[b, g][:])

        def plane_store(b, g):
            cols = slice(b * S, (b + 1) * S)
            nc.sync.dma_start(
                out=out_1[g, :, cols, :].rearrange("p n t -> p (n t)").bitcast(I32), in_=oq[b, g][:].bitcast(I32)
            )
            if g == 1:
                for q in range(4):
                    nc.sync.dma_start(
                        out=out_2[:, 4 * q : 4 * q + 4, cols].rearrange("g r n -> r g n").bitcast(I32),
                        in_=osc[b][32 * q : 32 * q + 4, :, :].bitcast(I32),
                    )

        every_tile = {
            "X": x_transpose, "xc": x_copy, "xq": x_quant, "F": f_mm, "y": mix, "mx": row_max, "ex": exp_sum,
            "rc": sum_recip, "w": normalise, "C": c_transpose, "cf": c_form, "cq": c_quant, "st": o_store,
            "H0": h_narrow, "H1": h_wide, "v0": v_narrow, "v1": v_wide, "il": v_interleave,
            "O0": lambda n: o_mm(n, 0), "O1": lambda n: o_mm(n, 1),
            "e0": lambda n: o_evac(n, 0), "e1": lambda n: o_evac(n, 1),
            "k0": lambda n: o_cast(n, 0), "k1": lambda n: o_cast(n, 1),
        }
        every_pair = {
            "T0": lambda n: o_transpose(n // 2, 0), "T1": lambda n: o_transpose(n // 2, 1),
            "og0": lambda n: o_gather(n // 2, 0), "og1": lambda n: o_gather(n // 2, 1),
        }
        every_batch = {
            "vq0": lambda b: v_quant(b, 0), "vq1": lambda b: v_quant(b, 1),
            "oq0": lambda b: o_quant(b, 0), "oq1": lambda b: o_quant(b, 1),
            "ps0": lambda b: plane_store(b, 0), "ps1": lambda b: plane_store(b, 1),
        }
        every_group = {"G": gate_mm, "gc": gate_clamp, "ge": gate_exp, "gd": gate_den, "gr": gate_recip}
        for s in range(NT + max(max(lags) for name, lags in STEP)):
            for name, lags in STEP:
                for n in range(NT):
                    if n + lags[n // PACK] != s:
                        continue
                    if name in every_tile:
                        every_tile[name](n)
                    elif name in every_pair and n % 2 == 1:
                        every_pair[name](n)
                    elif name in every_batch and n % PACK == PACK - 1:
                        every_batch[name](n // PACK)
                    elif name in every_group and n == group(n)[-1]:
                        every_group[name](n)
